import numpy as np
import ml_dtypes


def mxq(x, axis, fmt="e4m3"):
    dtype, down = {"e4m3": (ml_dtypes.float8_e4m3fn, 7), "e5m2": (ml_dtypes.float8_e5m2, 14)}[fmt]
    v = np.moveaxis(np.asarray(x, np.float32).astype(ml_dtypes.bfloat16).astype(np.float64), axis, -1)
    blocks = v.reshape(v.shape[:-1] + (-1, 32))
    amax = np.abs(blocks).max(-1, keepdims=True)
    byte = np.maximum(np.where(amax > 0, np.frexp(amax)[1] - 1 + 127, 0) - down, 1)
    scale = np.exp2(byte - 127.0)
    codes = (blocks / scale).astype(np.float32).astype(dtype).astype(np.float64)
    return np.moveaxis((codes * scale).reshape(v.shape), -1, axis)


WIDE = False


def mx_kscale(k):
    if not WIDE:
        return np.ones(k)
    levels = np.array([30, -30])
    if k % 512:
        return np.exp2(np.random.permutation(np.resize(levels, k // 32))).repeat(32)
    a = np.empty((k // 512, 16))
    for p in range(k // 512):
        a[p, :8] = np.random.permutation(np.resize(levels, 8))
        for g in range(8):
            far = levels[np.abs(levels - a[p, g]) >= 10]
            a[p, g + 8] = far[np.random.randint(len(far))]
    return np.exp2(a.ravel()).repeat(32)


BF16 = ml_dtypes.bfloat16


def bf(x):
    return np.asarray(x, np.float32).astype(BF16)


def f64(x):
    return np.asarray(x).astype(np.float64)


T, C, L, N = 2048, 1024, 2048, 512


def setup_inputs():
    s = mx_kscale(C)
    u = mx_kscale(L)
    heavy = np.random.standard_normal((T, L)) * np.exp(0.7 * np.random.standard_normal((T, L)))
    return {"frames": bf(np.random.standard_normal((T, C)) * s),
            "mel": bf(np.random.standard_normal((C, N)) / np.sqrt(C) / s[:, None]),
            "past": bf(heavy * u),
            "late": bf(-0.6 * np.random.standard_normal((L, N)) / np.sqrt(L) / u[:, None]),
            "bias": bf(0.3 * np.random.standard_normal(N)),
            "gain": bf(1 + 0.1 * np.random.standard_normal(N))}


def reference(frames, mel, past, late, bias, gain):
    x = mxq(f64(frames), 1, "e4m3")
    w = mxq(f64(mel), 0, "e4m3")
    d = mxq(f64(past), 1, "e5m2")
    g = mxq(f64(late), 0, "e4m3")
    y = (x @ w) + (d @ g)
    e = np.maximum(y + f64(bias), 0.0)
    return np.log(1.0 + f64(gain) * e)

@@ -1,0 +1,205 @@
+from contextlib import ExitStack
+
+import concourse.mybir as mybir
+from concourse.masks import make_identity
+
+T, C, L, N = 2048, 1024, 2048, 512
+FLOPS = 2 * T * (C + L) * N
+
+F32 = mybir.dt.float32
+BF16 = mybir.dt.bfloat16
+U32 = mybir.dt.uint32
+U8 = mybir.dt.uint8
+E4M3 = mybir.dt.float8_e4m3fn_x4
+E5M2 = mybir.dt.float8_e5m2_x4
+ALU = mybir.AluOpType
+ACT = mybir.ActivationFunctionType
+
+P = 128
+PACK = 4
+K_PASS = P * PACK
+TILES = T // P
+F_PASSES = C // K_PASS
+P_PASSES = L // K_PASS
+PASSES = F_PASSES + P_PASSES
+WORDS = K_PASS // 2
+V_COLS = 256
+RAW_BUFS = 8
+
+
+def tile_mel_dereverberation_s2_kernel(tc, frames, mel, past, late, bias, gain, out):
+    nc = tc.nc
+    with ExitStack() as ctx:
+        keep = ctx.enter_context(tc.tile_pool(name="keep", bufs=1))
+        raw = ctx.enter_context(tc.tile_pool(name="raw", bufs=RAW_BUFS))
+        work = ctx.enter_context(tc.tile_pool(name="work", bufs=3))
+        quant = ctx.enter_context(tc.tile_pool(name="quant", bufs=4))
+        turn = ctx.enter_context(tc.psum_pool(name="turn", bufs=6))
+        sums = ctx.enter_context(tc.psum_pool(name="sums", bufs=2))
+        ctx.enter_context(tc.manual_schedule())
+
+        ident = keep.tile([P, P], F32)
+        make_identity(nc, ident[:])
+
+        def load_band_vector(vec, name):
+            cols = keep.tile([P, PACK], BF16, name=name + "_cols")
+            nc.scalar.dma_start(out=cols[:], in_=vec.rearrange("(p c) -> p c", c=PACK))
+            return cols
+
+        def spread_band_vector(cols, name):
+            cols32 = keep.tile([P, PACK], F32, name=name + "_cols32")
+            nc.scalar.copy(out=cols32[:], in_=cols[:])
+            bank = turn.tile([P, PACK, P], F32, name="bank")
+            for c in range(PACK):
+                nc.tensor.transpose(bank[:, c, :], cols32[:, c : c + 1].to_broadcast([P, P]), ident[:])
+            rows = keep.tile([P, N], F32, name=name + "_rows")
+            nc.scalar.copy(out=rows[:].rearrange("r (p c) -> r p c", c=PACK), in_=bank[:].rearrange("r c p -> r p c"))
+            return rows
+
+        w_raw, w_grouped, w_codes, w_scales = {}, {}, {}, {}
+        f_raw, p_raw, p_sorted, f_grouped, p_grouped = {}, {}, {}, {}, {}
+        x_codes, acc, biased, gained, result = {}, {}, {}, {}, {}
+
+        def load_weight(g):
+            src, g0 = (mel, g) if g < F_PASSES else (late, g - F_PASSES)
+            w_raw[g] = keep.tile([P, PACK, N], BF16, name="w_raw%d" % g)
+            rows = src[g0 * K_PASS : (g0 + 1) * K_PASS, :]
+            nc.sync.dma_start(out=w_raw[g][:], in_=rows.rearrange("(p j) n -> p j n", j=PACK))
+
+        def group_weight(g):
+            w_grouped[g] = work.tile([P, N, PACK], BF16, name="w_grouped", align_bytes=64)
+            for copy, cols in ((nc.vector.tensor_copy, slice(0, V_COLS)), (nc.scalar.copy, slice(V_COLS, N))):
+                copy(
+                    out=w_grouped[g][:, cols, :].rearrange("p (c i) t -> p c t i", i=4),
+                    in_=w_raw[g][:, :, cols].rearrange("p t (c i) -> p c t i", i=4),
+                )
+
+        def quantize_weight(g):
+            w_codes[g] = keep.tile([P, N], U32, name="w_codes%d" % g, align_bytes=64)
+            w_scales[g] = keep.tile([P, N], U8, name="w_scales%d" % g, align_bytes=64)
+            nc.vector.quantize_mx(
+                out=w_codes[g][:].bitcast(E4M3),
+                scales=w_scales[g][:],
+                in_=w_grouped[g][:].rearrange("p n t -> p (n t)"),
+            )
+
+        def load_tokens(i):
+            rows = slice(i * P, (i + 1) * P)
+            p_raw[i] = raw.tile([P, L], BF16, name="p_raw")
+            nc.sync.dma_start(out=p_raw[i][:], in_=past[rows, :])
+            f_raw[i] = raw.tile([P, C], BF16, name="f_raw")
+            nc.sync.dma_start(out=f_raw[i][:], in_=frames[rows, :])
+
+        def sort_past(i):
+            p_sorted[i] = work.tile([P, P_PASSES, 2, P], F32, name="p_sorted")
+            words = p_raw[i][:].bitcast(F32)
+            nc.vector.tensor_copy(out=p_sorted[i][:], in_=words.rearrange("r (g m u) -> r g u m", g=P_PASSES, u=2))
+
+        def turn_tokens(i):
+            p_grouped[i] = work.tile([P, P_PASSES * K_PASS], BF16, name="p_grouped", align_bytes=64)
+            f_grouped[i] = work.tile([P, F_PASSES * K_PASS], BF16, name="f_grouped", align_bytes=64)
+            f_words = f_raw[i][:].bitcast(F32)
+            for g0 in range(0, PASSES, 2):
+                bank = turn.tile([P, 2, 2, P], F32, name="bank")
+                for g in range(2):
+                    for u in range(2):
+                        if g0 < P_PASSES:
+                            src = p_sorted[i][:, g0 + g, u, :]
+                        else:
+                            src = f_words[:, g * WORDS + u : (g + 1) * WORDS : 2]
+                        nc.tensor.transpose(bank[:, g, u, :], src, ident[:])
+                if g0 < P_PASSES:
+                    dst = p_grouped[i][:, g0 * K_PASS : (g0 + 2) * K_PASS]
+                else:
+                    dst = f_grouped[i][:]
+                nc.scalar.copy(
+                    out=dst.bitcast(F32).rearrange("p (g r u) -> p g r u", g=2, u=2),
+                    in_=bank[:].rearrange("p g u r -> p g r u"),
+                )
+
+        def quantize_tokens(i, grouped, passes, fmt, name):
+            codes = quant.tile([P, passes * P], U32, name=name + "_codes", align_bytes=64)
+            scales = quant.tile([P, passes * P], U8, name=name + "_scales", align_bytes=64)
+            nc.vector.quantize_mx(out=codes[:].bitcast(fmt), scales=scales[:], in_=grouped[i][:])
+            x_codes[i, name] = (codes, scales, fmt)
+
+        def multiply(i):
+            acc[i] = sums.tile([P, N], F32, name="acc")
+            for g in range(PASSES):
+                name, g0 = ("f", g) if g < F_PASSES else ("p", g - F_PASSES)
+                codes, scales, fmt = x_codes[i, name]
+                cols = slice(g0 * P, (g0 + 1) * P)
+                nc.tensor.matmul_mx(
+                    out=acc[i][:],
+                    lhsT=codes[:, cols].bitcast(fmt),
+                    lhsT_scale=scales[:, cols],
+                    rhs=w_codes[g][:].bitcast(E4M3),
+                    rhs_scale=w_scales[g][:],
+                    start=(g == 0),
+                    stop=(g == PASSES - 1),
+                )
+
+        def add_bias(i):
+            biased[i] = work.tile([P, N], F32, name="biased")
+            nc.vector.tensor_tensor(out=biased[i][:], in0=acc[i][:], in1=bias_rows[:], op=ALU.add)
+
+        def floor_and_gain(i):
+            gained[i] = work.tile([P, N], F32, name="gained")
+            nc.vector.scalar_tensor_tensor(
+                out=gained[i][:], in0=biased[i][:], scalar=0.0, in1=gain_rows[:], op0=ALU.max, op1=ALU.mult
+            )
+
+        def compress_and_store(i):
+            result[i] = quant.tile([P, N], F32, name="result")
+            nc.scalar.activation(out=result[i][:], in_=gained[i][:], func=ACT.Ln, bias=1.0)
+            nc.sync.dma_start(out=out[i * P : (i + 1) * P, :], in_=result[i][:])
+
+        bias_cols = load_band_vector(bias, "bias")
+        gain_cols = load_band_vector(gain, "gain")
+        load_weight(0)
+        load_weight(1)
+        load_tokens(0)
+        for g in range(2, PASSES):
+            load_weight(g)
+        for i in range(1, RAW_BUFS):
+            load_tokens(i)
+        bias_rows = spread_band_vector(bias_cols, "bias")
+        gain_rows = spread_band_vector(gain_cols, "gain")
+
+        group_weight(0)
+        group_weight(1)
+        quantize_weight(0)
+        sort_past(0)
+        quantize_weight(1)
+        turn_tokens(0)
+        group_weight(2)
+        for g in range(3, PASSES):
+            group_weight(g)
+            quantize_weight(g - 1)
+        quantize_tokens(0, f_grouped, F_PASSES, E4M3, "f")
+        quantize_weight(PASSES - 1)
+        quantize_tokens(0, p_grouped, P_PASSES, E5M2, "p")
+        sort_past(1)
+
+        def valid(i):
+            return 0 <= i < TILES
+
+        for s in range(1, TILES + 4):
+            if valid(s - 4):
+                compress_and_store(s - 4)
+            if valid(s + 1):
+                sort_past(s + 1)
+            if valid(s):
+                turn_tokens(s)
+            if valid(s - 1 + RAW_BUFS):
+                load_tokens(s - 1 + RAW_BUFS)
+            if valid(s - 3):
+                add_bias(s - 3)
+            if valid(s - 1) and s > 1:
+                quantize_tokens(s - 1, f_grouped, F_PASSES, E4M3, "f")
+            if valid(s - 3):
+                floor_and_gain(s - 3)
+            if valid(s - 1) and s > 1:
+                quantize_tokens(s - 1, p_grouped, P_PASSES, E5M2, "p")
+            if valid(s - 2):
+                multiply(s - 2)

@@ -19,12 +19,16 @@ P = 128
 PACK = 4
 K_PASS = P * PACK
 TILES = T // P
-F_PASSES = C // K_PASS
-P_PASSES = L // K_PASS
-PASSES = F_PASSES + P_PASSES
+CHUNK = 2 * K_PASS
+CHUNKS = (C + L) // CHUNK
+PASSES = 2 * CHUNKS
 WORDS = K_PASS // 2
-V_COLS = 256
-RAW_BUFS = 8
+V_COLS = 384
+RAW_BUFS = 6
+HEAD = 4
+SORT_FROM = 6
+S_SORT_FROM = 6
+TAIL_PARTS = 2
 
 
 def tile_mel_dereverberation_s2_kernel(tc, frames, mel, past, late, bias, gain, out):
@@ -34,45 +38,36 @@ def tile_mel_dereverberation_s2_kernel(tc, frames, mel, past, late, bias, gain, 
         raw = ctx.enter_context(tc.tile_pool(name="raw", bufs=RAW_BUFS))
         work = ctx.enter_context(tc.tile_pool(name="work", bufs=3))
         quant = ctx.enter_context(tc.tile_pool(name="quant", bufs=4))
-        turn = ctx.enter_context(tc.psum_pool(name="turn", bufs=6))
-        sums = ctx.enter_context(tc.psum_pool(name="sums", bufs=2))
+        turn = ctx.enter_context(tc.psum_pool(name="turn", bufs=4))
+        sums = ctx.enter_context(tc.psum_pool(name="sums", bufs=4))
         ctx.enter_context(tc.manual_schedule())
 
         ident = keep.tile([P, P], F32)
         make_identity(nc, ident[:])
 
-        def load_band_vector(vec, name):
-            cols = keep.tile([P, PACK], BF16, name=name + "_cols")
-            nc.scalar.dma_start(out=cols[:], in_=vec.rearrange("(p c) -> p c", c=PACK))
-            return cols
-
-        def spread_band_vector(cols, name):
-            cols32 = keep.tile([P, PACK], F32, name=name + "_cols32")
-            nc.scalar.copy(out=cols32[:], in_=cols[:])
-            bank = turn.tile([P, PACK, P], F32, name="bank")
-            for c in range(PACK):
-                nc.tensor.transpose(bank[:, c, :], cols32[:, c : c + 1].to_broadcast([P, P]), ident[:])
-            rows = keep.tile([P, N], F32, name=name + "_rows")
-            nc.scalar.copy(out=rows[:].rearrange("r (p c) -> r p c", c=PACK), in_=bank[:].rearrange("r c p -> r p c"))
-            return rows
-
         w_raw, w_grouped, w_codes, w_scales = {}, {}, {}, {}
-        f_raw, p_raw, p_sorted, f_grouped, p_grouped = {}, {}, {}, {}, {}
-        x_codes, acc, biased, gained, result = {}, {}, {}, {}, {}
+        x_raw, x_words, x_grouped, x_codes, x_scales = {}, {}, {}, {}, {}
+        acc, biased, gained = {}, {}, {}
+
+        def source(j):
+            return (frames, 0) if j == 0 else (past, (j - 1) * CHUNK)
+
+        def x_format(j):
+            return E4M3 if j == 0 else E5M2
 
         def load_weight(g):
-            src, g0 = (mel, g) if g < F_PASSES else (late, g - F_PASSES)
+            src, g0 = (mel, g) if g < 2 else (late, g - 2)
             w_raw[g] = keep.tile([P, PACK, N], BF16, name="w_raw%d" % g)
             rows = src[g0 * K_PASS : (g0 + 1) * K_PASS, :]
             nc.sync.dma_start(out=w_raw[g][:], in_=rows.rearrange("(p j) n -> p j n", j=PACK))
 
-        def group_weight(g):
-            w_grouped[g] = work.tile([P, N, PACK], BF16, name="w_grouped", align_bytes=64)
-            for copy, cols in ((nc.vector.tensor_copy, slice(0, V_COLS)), (nc.scalar.copy, slice(V_COLS, N))):
-                copy(
-                    out=w_grouped[g][:, cols, :].rearrange("p (c i) t -> p c t i", i=4),
-                    in_=w_raw[g][:, :, cols].rearrange("p t (c i) -> p c t i", i=4),
-                )
+        def group_weight(g, copy, cols):
+            if g not in w_grouped:
+                w_grouped[g] = work.tile([P, N, PACK], BF16, name="w_grouped", align_bytes=64)
+            copy(
+                out=w_grouped[g][:, cols, :].rearrange("p (c i) t -> p c t i", i=4),
+                in_=w_raw[g][:, :, cols].rearrange("p t (c i) -> p c t i", i=4),
+            )
 
         def quantize_weight(g):
             w_codes[g] = keep.tile([P, N], U32, name="w_codes%d" % g, align_bytes=64)
@@ -83,123 +78,203 @@ def tile_mel_dereverberation_s2_kernel(tc, frames, mel, past, late, bias, gain, 
                 in_=w_grouped[g][:].rearrange("p n t -> p (n t)"),
             )
 
+        def load_pair(r):
+            i0, j = 2 * (r % 2), r // 2
+            src, k0 = source(j)
+            pair = keep.tile([P, 2, CHUNK], BF16, name="pair%d" % r)
+            rows = src[i0 * P : (i0 + 2) * P, k0 : k0 + CHUNK]
+            nc.sync.dma_start(out=pair[:], in_=rows.rearrange("(i r) k -> r i k", i=2))
+            for i in range(2):
+                x_raw[i0 + i, j] = pair[:, i, :]
+
         def load_tokens(i):
             rows = slice(i * P, (i + 1) * P)
-            p_raw[i] = raw.tile([P, L], BF16, name="p_raw")
-            nc.sync.dma_start(out=p_raw[i][:], in_=past[rows, :])
-            f_raw[i] = raw.tile([P, C], BF16, name="f_raw")
-            nc.sync.dma_start(out=f_raw[i][:], in_=frames[rows, :])
+            p_raw = raw.tile([P, L], BF16, name="p_raw")
+            nc.sync.dma_start(out=p_raw[:], in_=past[rows, :])
+            f_raw = raw.tile([P, C], BF16, name="f_raw")
+            nc.sync.dma_start(out=f_raw[:], in_=frames[rows, :])
+            x_raw[i, 0] = f_raw[:]
+            x_raw[i, 1] = p_raw[:, :CHUNK]
+            x_raw[i, 2] = p_raw[:, CHUNK:]
+            x_raw[i, "past"] = p_raw[:]
 
         def sort_past(i):
-            p_sorted[i] = work.tile([P, P_PASSES, 2, P], F32, name="p_sorted")
-            words = p_raw[i][:].bitcast(F32)
-            nc.vector.tensor_copy(out=p_sorted[i][:], in_=words.rearrange("r (g m u) -> r g u m", g=P_PASSES, u=2))
+            ordered = work.tile([P, 4, 2, P], F32, name="p_sorted")
+            words = x_raw[i, "past"].bitcast(F32)
+            nc.vector.tensor_copy(out=ordered[:], in_=words.rearrange("r (g m u) -> r g u m", g=4, u=2))
+            x_words[i, 1] = ordered[:, 0:2, :, :]
+            x_words[i, 2] = ordered[:, 2:4, :, :]
 
-        def turn_tokens(i):
-            p_grouped[i] = work.tile([P, P_PASSES * K_PASS], BF16, name="p_grouped", align_bytes=64)
-            f_grouped[i] = work.tile([P, F_PASSES * K_PASS], BF16, name="f_grouped", align_bytes=64)
-            f_words = f_raw[i][:].bitcast(F32)
-            for g0 in range(0, PASSES, 2):
-                bank = turn.tile([P, 2, 2, P], F32, name="bank")
-                for g in range(2):
-                    for u in range(2):
-                        if g0 < P_PASSES:
-                            src = p_sorted[i][:, g0 + g, u, :]
-                        else:
-                            src = f_words[:, g * WORDS + u : (g + 1) * WORDS : 2]
-                        nc.tensor.transpose(bank[:, g, u, :], src, ident[:])
-                if g0 < P_PASSES:
-                    dst = p_grouped[i][:, g0 * K_PASS : (g0 + 2) * K_PASS]
-                else:
-                    dst = f_grouped[i][:]
-                nc.scalar.copy(
-                    out=dst.bitcast(F32).rearrange("p (g r u) -> p g r u", g=2, u=2),
-                    in_=bank[:].rearrange("p g u r -> p g r u"),
-                )
+        def sort_frames(i):
+            ordered = work.tile([P, 2, 2, P], F32, name="f_sorted")
+            words = x_raw[i, 0].bitcast(F32)
+            nc.scalar.copy(out=ordered[:], in_=words.rearrange("r (g m u) -> r g u m", g=2, u=2))
+            x_words[i, 0] = ordered[:]
 
-        def quantize_tokens(i, grouped, passes, fmt, name):
-            codes = quant.tile([P, passes * P], U32, name=name + "_codes", align_bytes=64)
-            scales = quant.tile([P, passes * P], U8, name=name + "_scales", align_bytes=64)
-            nc.vector.quantize_mx(out=codes[:].bitcast(fmt), scales=scales[:], in_=grouped[i][:])
-            x_codes[i, name] = (codes, scales, fmt)
-
-        def multiply(i):
-            acc[i] = sums.tile([P, N], F32, name="acc")
-            for g in range(PASSES):
-                name, g0 = ("f", g) if g < F_PASSES else ("p", g - F_PASSES)
-                codes, scales, fmt = x_codes[i, name]
-                cols = slice(g0 * P, (g0 + 1) * P)
-                nc.tensor.matmul_mx(
-                    out=acc[i][:],
-                    lhsT=codes[:, cols].bitcast(fmt),
-                    lhsT_scale=scales[:, cols],
-                    rhs=w_codes[g][:].bitcast(E4M3),
-                    rhs_scale=w_scales[g][:],
-                    start=(g == 0),
-                    stop=(g == PASSES - 1),
-                )
-
-        def add_bias(i):
-            biased[i] = work.tile([P, N], F32, name="biased")
-            nc.vector.tensor_tensor(out=biased[i][:], in0=acc[i][:], in1=bias_rows[:], op=ALU.add)
-
-        def floor_and_gain(i):
-            gained[i] = work.tile([P, N], F32, name="gained")
-            nc.vector.scalar_tensor_tensor(
-                out=gained[i][:], in0=biased[i][:], scalar=0.0, in1=gain_rows[:], op0=ALU.max, op1=ALU.mult
+        def turn_chunk(i, j):
+            if (i, j) in x_words:
+                words = x_words[i, j]
+            else:
+                words = x_raw[i, j].bitcast(F32).rearrange("r (g m u) -> r g u m", g=2, u=2)
+            bank = turn.tile([P, 2, 2, P], F32, name="bank")
+            for g in range(2):
+                for u in range(2):
+                    nc.tensor.transpose(bank[:, g, u, :], words[:, g, u, :], ident[:])
+            if i < HEAD or j == 0:
+                grouped = work.tile([P, CHUNK], BF16, name="grouped", align_bytes=64, bufs=4)
+                x_grouped[i, j] = grouped[:]
+            elif j == 1:
+                grouped = work.tile([P, L], BF16, name="p_grouped", align_bytes=64)
+                x_grouped[i, "past"] = grouped[:]
+                x_grouped[i, 1] = grouped[:, :CHUNK]
+                x_grouped[i, 2] = grouped[:, CHUNK:]
+            nc.scalar.copy(
+                out=x_grouped[i, j].bitcast(F32).rearrange("p (g r u) -> p g r u", g=2, u=2),
+                in_=bank[:].rearrange("p g u r -> p g r u"),
             )
 
-        def compress_and_store(i):
-            result[i] = quant.tile([P, N], F32, name="result")
-            nc.scalar.activation(out=result[i][:], in_=gained[i][:], func=ACT.Ln, bias=1.0)
-            nc.sync.dma_start(out=out[i * P : (i + 1) * P, :], in_=result[i][:])
+        def quantize_chunk(i, j):
+            codes = quant.tile([P, 2 * P], U32, name="codes", align_bytes=64, bufs=8)
+            scales = quant.tile([P, 2 * P], U8, name="scales", align_bytes=64, bufs=8)
+            nc.vector.quantize_mx(out=codes[:].bitcast(x_format(j)), scales=scales[:], in_=x_grouped[i, j])
+            for g in range(2):
+                x_codes[i, 2 * j + g] = codes[:, g * P : (g + 1) * P]
+                x_scales[i, 2 * j + g] = scales[:, g * P : (g + 1) * P]
 
-        bias_cols = load_band_vector(bias, "bias")
-        gain_cols = load_band_vector(gain, "gain")
-        load_weight(0)
-        load_weight(1)
-        load_tokens(0)
-        for g in range(2, PASSES):
-            load_weight(g)
-        for i in range(1, RAW_BUFS):
+        def quantize_past(i):
+            codes = quant.tile([P, 4 * P], U32, name="p_codes", align_bytes=64)
+            scales = quant.tile([P, 4 * P], U8, name="p_scales", align_bytes=64)
+            nc.vector.quantize_mx(out=codes[:].bitcast(E5M2), scales=scales[:], in_=x_grouped[i, "past"])
+            for g in range(4):
+                x_codes[i, 2 + g] = codes[:, g * P : (g + 1) * P]
+                x_scales[i, 2 + g] = scales[:, g * P : (g + 1) * P]
+
+        def multiply(i, g):
+            if g == 0:
+                acc[i] = sums.tile([P, N], F32, name="acc")
+            nc.tensor.matmul_mx(
+                out=acc[i][:],
+                lhsT=x_codes[i, g].bitcast(x_format(g // 2)),
+                lhsT_scale=x_scales[i, g],
+                rhs=w_codes[g][:].bitcast(E4M3),
+                rhs_scale=w_scales[g][:],
+                start=(g == 0),
+                stop=(g == PASSES - 1),
+            )
+
+        def add_bias(i, cols):
+            if i not in biased:
+                biased[i] = work.tile([P, N], F32, name="biased")
+            nc.vector.tensor_tensor(out=biased[i][:, cols], in0=acc[i][:, cols], in1=bias_rows[:, cols], op=ALU.add)
+
+        def floor_and_gain(i, cols):
+            if i not in gained:
+                gained[i] = work.tile([P, N], F32, name="gained")
+            nc.vector.scalar_tensor_tensor(
+                out=gained[i][:, cols], in0=biased[i][:, cols], scalar=0.0, in1=gain_rows[:, cols], op0=ALU.max, op1=ALU.mult
+            )
+
+        def compress_and_store(i, cols):
+            width = cols.stop - cols.start
+            result = quant.tile([P, width], F32, name="result")
+            nc.scalar.activation(out=result[:], in_=gained[i][:, cols], func=ACT.Ln, bias=1.0)
+            nc.sync.dma_start(out=out[i * P : (i + 1) * P, cols], in_=result[:])
+
+        bias_cols = keep.tile([P, PACK], BF16)
+        nc.scalar.dma_start(out=bias_cols[:], in_=bias.rearrange("(p c) -> p c", c=PACK))
+        gain_cols = keep.tile([P, PACK], BF16)
+        nc.scalar.dma_start(out=gain_cols[:], in_=gain.rearrange("(p c) -> p c", c=PACK))
+        warm = keep.tile([P, 1], F32)
+        nc.vector.memset(warm[:], 0.0)
+        nc.scalar.activation(out=warm[:], in_=warm[:], func=ACT.Ln, bias=1.0)
+
+        for r in range(PASSES):
+            load_pair(r)
+            if r == PASSES - 1 and False:
+                load_tokens(HEAD)
+            load_weight(r)
+        for i in range(HEAD + 0, HEAD + RAW_BUFS):
             load_tokens(i)
-        bias_rows = spread_band_vector(bias_cols, "bias")
-        gain_rows = spread_band_vector(gain_cols, "gain")
 
-        group_weight(0)
-        group_weight(1)
-        quantize_weight(0)
-        sort_past(0)
-        quantize_weight(1)
-        turn_tokens(0)
-        group_weight(2)
-        for g in range(3, PASSES):
-            group_weight(g)
-            quantize_weight(g - 1)
-        quantize_tokens(0, f_grouped, F_PASSES, E4M3, "f")
-        quantize_weight(PASSES - 1)
-        quantize_tokens(0, p_grouped, P_PASSES, E5M2, "p")
-        sort_past(1)
+        band_rows = []
+        for name, cols in (("bias", bias_cols), ("gain", gain_cols)):
+            cols32 = keep.tile([P, PACK], F32, name=name + "_cols32")
+            nc.scalar.copy(out=cols32[:], in_=cols[:])
+            bank = turn.tile([P, PACK, P], F32, name="bank")
+            for c in range(PACK):
+                nc.tensor.transpose(bank[:, c, :], cols32[:, c : c + 1].to_broadcast([P, P]), ident[:])
+            rows = keep.tile([P, N], F32, name=name + "_rows")
+            nc.vector.tensor_copy(out=rows[:].rearrange("r (p c) -> r p c", c=PACK), in_=bank[:].rearrange("r c p -> r p c"))
+            band_rows.append(rows)
+        bias_rows, gain_rows = band_rows
 
-        def valid(i):
-            return 0 <= i < TILES
+        def head_multiply(r):
+            for i0, g in ((2, r - 1), (0, r)):
+                if 0 <= g < PASSES:
+                    multiply(i0, g)
+                    multiply(i0 + 1, g)
 
-        for s in range(1, TILES + 4):
-            if valid(s - 4):
-                compress_and_store(s - 4)
-            if valid(s + 1):
-                sort_past(s + 1)
-            if valid(s):
-                turn_tokens(s)
-            if valid(s - 1 + RAW_BUFS):
-                load_tokens(s - 1 + RAW_BUFS)
-            if valid(s - 3):
-                add_bias(s - 3)
-            if valid(s - 1) and s > 1:
-                quantize_tokens(s - 1, f_grouped, F_PASSES, E4M3, "f")
-            if valid(s - 3):
-                floor_and_gain(s - 3)
-            if valid(s - 1) and s > 1:
-                quantize_tokens(s - 1, p_grouped, P_PASSES, E5M2, "p")
-            if valid(s - 2):
-                multiply(s - 2)
+        def sorts(i):
+            if SORT_FROM <= i < TILES:
+                sort_past(i)
+        def ssorts(i):
+            if S_SORT_FROM <= i < TILES:
+                sort_frames(i)
+
+        for r in range(PASSES):
+            i0, j = 2 * (r % 2), r // 2
+            turn_chunk(i0, j)
+            turn_chunk(i0 + 1, j)
+            if r > 0:
+                head_multiply(r - 1)
+            if r == PASSES - 1:
+                quantize_chunk(i0, j)
+                sorts(HEAD)
+                ssorts(HEAD)
+                quantize_chunk(i0 + 1, j)
+            group_weight(r, nc.vector.tensor_copy, slice(0, V_COLS))
+            group_weight(r, nc.scalar.copy, slice(V_COLS, N))
+            if r < PASSES - 1:
+                quantize_chunk(i0, j)
+                quantize_chunk(i0 + 1, j)
+            quantize_weight(r)
+
+        whole = slice(0, N)
+        finish_at = lambda i: max(i + 3, 5 + i // 2)
+        for s in range(HEAD, TILES + 3):
+            done = [i for i in range(TILES - 1) if finish_at(i) == s]
+            late_done = [i for i in range(TILES - 1) if finish_at(i) == s - 1]
+            if True:
+                for i in late_done:
+                    compress_and_store(i, whole)
+            sorts(s + 1)
+            if s < TILES:
+                for j in (1, 2, 0):
+                    turn_chunk(s, j)
+            if not True:
+                for i in late_done:
+                    compress_and_store(i, whole)
+            ssorts(s + 1)
+            if s + RAW_BUFS < TILES:
+                load_tokens(s + RAW_BUFS)
+            for i in done:
+                add_bias(i, whole)
+            if HEAD <= s - 1 < TILES:
+                quantize_chunk(s - 1, 0)
+            for i in done:
+                floor_and_gain(i, whole)
+            if HEAD <= s - 1 < TILES:
+                quantize_past(s - 1)
+            if s - 2 < HEAD:
+                head_multiply(s + 1)
+            elif s - 2 < TILES:
+                for g in range(PASSES):
+                    multiply(s - 2, g)
+        last = TILES - 1
+        parts = [slice(a * N // TAIL_PARTS, (a + 1) * N // TAIL_PARTS) for a in range(TAIL_PARTS)]
+        for a in range(TAIL_PARTS + 1):
+            if a < TAIL_PARTS:
+                add_bias(last, parts[a])
+            if a > 0:
+                floor_and_gain(last, parts[a - 1])
+                compress_and_store(last, parts[a - 1])

@@ -19,55 +19,59 @@ P = 128
 PACK = 4
 K_PASS = P * PACK
 TILES = T // P
-CHUNK = 2 * K_PASS
-CHUNKS = (C + L) // CHUNK
-PASSES = 2 * CHUNKS
-WORDS = K_PASS // 2
-V_COLS = 384
-RAW_BUFS = 6
+PAIRS = TILES // 2
+F_PASSES = C // K_PASS
+P_PASSES = L // K_PASS
+PASSES = F_PASSES + P_PASSES
 HEAD = 4
-SORT_FROM = 6
-S_SORT_FROM = 6
-TAIL_PARTS = 2
+V_BANDS = 384
+RAW_PAIRS = 4
+RESULT_BUFS = 8
+SORT_PAST_FROM = 5
+SORT_FRAMES_FROM = 8
+CATCH_UP = 6
+TAIL_PARTS = 4
 
 
 def tile_mel_dereverberation_s2_kernel(tc, frames, mel, past, late, bias, gain, out):
     nc = tc.nc
+    frames_by_pair = frames.rearrange("(q r s) k -> q r s k", r=P, s=2)
+    past_by_pair = past.rearrange("(q r s) k -> q r s k", r=P, s=2)
+    out_by_pair = out.rearrange("(q r s) n -> q r s n", r=P, s=2)
+
     with ExitStack() as ctx:
         keep = ctx.enter_context(tc.tile_pool(name="keep", bufs=1))
-        raw = ctx.enter_context(tc.tile_pool(name="raw", bufs=RAW_BUFS))
-        work = ctx.enter_context(tc.tile_pool(name="work", bufs=3))
-        quant = ctx.enter_context(tc.tile_pool(name="quant", bufs=4))
-        turn = ctx.enter_context(tc.psum_pool(name="turn", bufs=4))
-        sums = ctx.enter_context(tc.psum_pool(name="sums", bufs=4))
+        raw = ctx.enter_context(tc.tile_pool(name="raw", bufs=RAW_PAIRS))
+        work = ctx.enter_context(tc.tile_pool(name="work", bufs=4))
+        outs = ctx.enter_context(tc.tile_pool(name="outs", bufs=RESULT_BUFS))
+        turns = ctx.enter_context(tc.psum_pool(name="turns", bufs=4))
+        sums = ctx.enter_context(tc.psum_pool(name="sums", bufs=HEAD))
         ctx.enter_context(tc.manual_schedule())
 
         ident = keep.tile([P, P], F32)
         make_identity(nc, ident[:])
 
         w_raw, w_grouped, w_codes, w_scales = {}, {}, {}, {}
-        x_raw, x_words, x_grouped, x_codes, x_scales = {}, {}, {}, {}, {}
+        f_words, p_words, f_grouped, p_grouped = {}, {}, {}, {}
+        x_codes, x_scales = {}, {}
         acc, biased, gained = {}, {}, {}
 
-        def source(j):
-            return (frames, 0) if j == 0 else (past, (j - 1) * CHUNK)
-
-        def x_format(j):
-            return E4M3 if j == 0 else E5M2
+        def token_format(g):
+            return E4M3 if g < F_PASSES else E5M2
 
         def load_weight(g):
-            src, g0 = (mel, g) if g < 2 else (late, g - 2)
+            src, g_src = (mel, g) if g < F_PASSES else (late, g - F_PASSES)
+            rows = src[g_src * K_PASS : (g_src + 1) * K_PASS, :]
             w_raw[g] = keep.tile([P, PACK, N], BF16, name="w_raw%d" % g)
-            rows = src[g0 * K_PASS : (g0 + 1) * K_PASS, :]
-            nc.sync.dma_start(out=w_raw[g][:], in_=rows.rearrange("(p j) n -> p j n", j=PACK))
+            nc.sync.dma_start(out=w_raw[g][:], in_=rows.rearrange("(p t) n -> p t n", t=PACK))
 
-        def group_weight(g, copy, cols):
-            if g not in w_grouped:
-                w_grouped[g] = work.tile([P, N, PACK], BF16, name="w_grouped", align_bytes=64)
-            copy(
-                out=w_grouped[g][:, cols, :].rearrange("p (c i) t -> p c t i", i=4),
-                in_=w_raw[g][:, :, cols].rearrange("p t (c i) -> p c t i", i=4),
-            )
+        def group_weight(g):
+            w_grouped[g] = work.tile([P, N, PACK], BF16, name="w_grouped", align_bytes=64, bufs=2)
+            for copy, bands in ((nc.vector.tensor_copy, slice(0, V_BANDS)), (nc.scalar.copy, slice(V_BANDS, N))):
+                copy(
+                    out=w_grouped[g][:, bands, :].rearrange("p (c i) t -> p c t i", i=4),
+                    in_=w_raw[g][:, :, bands].rearrange("p t (c i) -> p c t i", i=4),
+                )
 
         def quantize_weight(g):
             w_codes[g] = keep.tile([P, N], U32, name="w_codes%d" % g, align_bytes=64)
@@ -78,83 +82,74 @@ def tile_mel_dereverberation_s2_kernel(tc, frames, mel, past, late, bias, gain, 
                 in_=w_grouped[g][:].rearrange("p n t -> p (n t)"),
             )
 
-        def load_pair(r):
-            i0, j = 2 * (r % 2), r // 2
-            src, k0 = source(j)
-            pair = keep.tile([P, 2, CHUNK], BF16, name="pair%d" % r)
-            rows = src[i0 * P : (i0 + 2) * P, k0 : k0 + CHUNK]
-            nc.sync.dma_start(out=pair[:], in_=rows.rearrange("(i r) k -> r i k", i=2))
-            for i in range(2):
-                x_raw[i0 + i, j] = pair[:, i, :]
+        def words_by_parity(rows):
+            return rows.bitcast(F32).rearrange("r (g m u) -> r g u m", m=P, u=2)
 
-        def load_tokens(i):
-            rows = slice(i * P, (i + 1) * P)
-            p_raw = raw.tile([P, L], BF16, name="p_raw")
-            nc.sync.dma_start(out=p_raw[:], in_=past[rows, :])
-            f_raw = raw.tile([P, C], BF16, name="f_raw")
-            nc.sync.dma_start(out=f_raw[:], in_=frames[rows, :])
-            x_raw[i, 0] = f_raw[:]
-            x_raw[i, 1] = p_raw[:, :CHUNK]
-            x_raw[i, 2] = p_raw[:, CHUNK:]
-            x_raw[i, "past"] = p_raw[:]
+        def load_frames(q):
+            f_raw = raw.tile([P, 2, C], BF16, name="f_raw")
+            nc.sync.dma_start(out=f_raw[:], in_=frames_by_pair[q])
+            for s in range(2):
+                f_words[2 * q + s] = words_by_parity(f_raw[:, s, :])
+
+        def load_past(i):
+            p_raw = raw.tile([P, L], BF16, name="p_raw", bufs=2 * RAW_PAIRS)
+            nc.sync.dma_start(out=p_raw[:], in_=past_by_pair[i // 2, :, i % 2, :])
+            p_words[i] = words_by_parity(p_raw[:])
+
+        def load_pair(q):
+            load_past(2 * q)
+            load_frames(q)
+            load_past(2 * q + 1)
 
         def sort_past(i):
-            ordered = work.tile([P, 4, 2, P], F32, name="p_sorted")
-            words = x_raw[i, "past"].bitcast(F32)
-            nc.vector.tensor_copy(out=ordered[:], in_=words.rearrange("r (g m u) -> r g u m", g=4, u=2))
-            x_words[i, 1] = ordered[:, 0:2, :, :]
-            x_words[i, 2] = ordered[:, 2:4, :, :]
+            p_sorted = work.tile([P, P_PASSES, 2, P], F32, name="p_sorted")
+            nc.vector.tensor_copy(out=p_sorted[:], in_=p_words[i])
+            p_words[i] = p_sorted[:]
 
         def sort_frames(i):
-            ordered = work.tile([P, 2, 2, P], F32, name="f_sorted")
-            words = x_raw[i, 0].bitcast(F32)
-            nc.scalar.copy(out=ordered[:], in_=words.rearrange("r (g m u) -> r g u m", g=2, u=2))
-            x_words[i, 0] = ordered[:]
+            f_sorted = work.tile([P, F_PASSES, 2, P], F32, name="f_sorted")
+            nc.scalar.copy(out=f_sorted[:], in_=f_words[i])
+            f_words[i] = f_sorted[:]
 
-        def turn_chunk(i, j):
-            if (i, j) in x_words:
-                words = x_words[i, j]
-            else:
-                words = x_raw[i, j].bitcast(F32).rearrange("r (g m u) -> r g u m", g=2, u=2)
-            bank = turn.tile([P, 2, 2, P], F32, name="bank")
+        def turn_two_passes(words, grouped):
+            bank = turns.tile([P, 2, 2, P], F32, name="bank")
             for g in range(2):
                 for u in range(2):
                     nc.tensor.transpose(bank[:, g, u, :], words[:, g, u, :], ident[:])
-            if i < HEAD or j == 0:
-                grouped = work.tile([P, CHUNK], BF16, name="grouped", align_bytes=64, bufs=4)
-                x_grouped[i, j] = grouped[:]
-            elif j == 1:
-                grouped = work.tile([P, L], BF16, name="p_grouped", align_bytes=64)
-                x_grouped[i, "past"] = grouped[:]
-                x_grouped[i, 1] = grouped[:, :CHUNK]
-                x_grouped[i, 2] = grouped[:, CHUNK:]
             nc.scalar.copy(
-                out=x_grouped[i, j].bitcast(F32).rearrange("p (g r u) -> p g r u", g=2, u=2),
+                out=grouped.bitcast(F32).rearrange("p (g r u) -> p g r u", g=2, u=2),
                 in_=bank[:].rearrange("p g u r -> p g r u"),
             )
 
-        def quantize_chunk(i, j):
-            codes = quant.tile([P, 2 * P], U32, name="codes", align_bytes=64, bufs=8)
-            scales = quant.tile([P, 2 * P], U8, name="scales", align_bytes=64, bufs=8)
-            nc.vector.quantize_mx(out=codes[:].bitcast(x_format(j)), scales=scales[:], in_=x_grouped[i, j])
-            for g in range(2):
-                x_codes[i, 2 * j + g] = codes[:, g * P : (g + 1) * P]
-                x_scales[i, 2 * j + g] = scales[:, g * P : (g + 1) * P]
+        def turn_frames(i):
+            f_grouped[i] = work.tile([P, C], BF16, name="f_grouped", align_bytes=64, bufs=3)
+            turn_two_passes(f_words[i], f_grouped[i][:])
+
+        def turn_past(i):
+            p_grouped[i] = work.tile([P, L], BF16, name="p_grouped", align_bytes=64, bufs=3)
+            for g in range(0, P_PASSES, 2):
+                turn_two_passes(p_words[i][:, g : g + 2, :, :], p_grouped[i][:, g * K_PASS : (g + 2) * K_PASS])
+
+        def quantize_tokens(i, grouped, first_pass, passes, name):
+            codes = work.tile([P, passes * P], U32, name=name + "_codes", align_bytes=64)
+            scales = work.tile([P, passes * P], U8, name=name + "_scales", align_bytes=64)
+            nc.vector.quantize_mx(out=codes[:].bitcast(token_format(first_pass)), scales=scales[:], in_=grouped[:])
+            for g in range(passes):
+                x_codes[i, first_pass + g] = codes[:, g * P : (g + 1) * P]
+                x_scales[i, first_pass + g] = scales[:, g * P : (g + 1) * P]
+
+        def quantize_frames(i):
+            quantize_tokens(i, f_grouped[i], 0, F_PASSES, "f")
 
         def quantize_past(i):
-            codes = quant.tile([P, 4 * P], U32, name="p_codes", align_bytes=64)
-            scales = quant.tile([P, 4 * P], U8, name="p_scales", align_bytes=64)
-            nc.vector.quantize_mx(out=codes[:].bitcast(E5M2), scales=scales[:], in_=x_grouped[i, "past"])
-            for g in range(4):
-                x_codes[i, 2 + g] = codes[:, g * P : (g + 1) * P]
-                x_scales[i, 2 + g] = scales[:, g * P : (g + 1) * P]
+            quantize_tokens(i, p_grouped[i], F_PASSES, P_PASSES, "p")
 
         def multiply(i, g):
             if g == 0:
                 acc[i] = sums.tile([P, N], F32, name="acc")
             nc.tensor.matmul_mx(
                 out=acc[i][:],
-                lhsT=x_codes[i, g].bitcast(x_format(g // 2)),
+                lhsT=x_codes[i, g].bitcast(token_format(g)),
                 lhsT_scale=x_scales[i, g],
                 rhs=w_codes[g][:].bitcast(E4M3),
                 rhs_scale=w_scales[g][:],
@@ -162,115 +157,122 @@ def tile_mel_dereverberation_s2_kernel(tc, frames, mel, past, late, bias, gain, 
                 stop=(g == PASSES - 1),
             )
 
-        def add_bias(i, cols):
-            if i not in biased:
+        def add_bias(i, bands):
+            if bands.start == 0:
                 biased[i] = work.tile([P, N], F32, name="biased")
-            nc.vector.tensor_tensor(out=biased[i][:, cols], in0=acc[i][:, cols], in1=bias_rows[:, cols], op=ALU.add)
+            nc.vector.tensor_tensor(out=biased[i][:, bands], in0=acc[i][:, bands], in1=bias_rows[:, bands], op=ALU.add)
 
-        def floor_and_gain(i, cols):
-            if i not in gained:
+        def floor_and_gain(i, bands):
+            if bands.start == 0:
                 gained[i] = work.tile([P, N], F32, name="gained")
             nc.vector.scalar_tensor_tensor(
-                out=gained[i][:, cols], in0=biased[i][:, cols], scalar=0.0, in1=gain_rows[:, cols], op0=ALU.max, op1=ALU.mult
+                out=gained[i][:, bands],
+                in0=biased[i][:, bands],
+                scalar=0.0,
+                in1=gain_rows[:, bands],
+                op0=ALU.max,
+                op1=ALU.mult,
             )
 
-        def compress_and_store(i, cols):
-            width = cols.stop - cols.start
-            result = quant.tile([P, width], F32, name="result")
-            nc.scalar.activation(out=result[:], in_=gained[i][:, cols], func=ACT.Ln, bias=1.0)
-            nc.sync.dma_start(out=out[i * P : (i + 1) * P, cols], in_=result[:])
+        def compress_and_store(i, bands):
+            result = outs.tile([P, bands.stop - bands.start], F32, name="result")
+            nc.scalar.activation(out=result[:], in_=gained[i][:, bands], func=ACT.Ln, bias=1.0)
+            nc.sync.dma_start(out=out_by_pair[i // 2, :, i % 2, bands], in_=result[:])
 
         bias_cols = keep.tile([P, PACK], BF16)
         nc.scalar.dma_start(out=bias_cols[:], in_=bias.rearrange("(p c) -> p c", c=PACK))
         gain_cols = keep.tile([P, PACK], BF16)
         nc.scalar.dma_start(out=gain_cols[:], in_=gain.rearrange("(p c) -> p c", c=PACK))
+
         warm = keep.tile([P, 1], F32)
         nc.vector.memset(warm[:], 0.0)
         nc.scalar.activation(out=warm[:], in_=warm[:], func=ACT.Ln, bias=1.0)
 
         for r in range(PASSES):
-            load_pair(r)
-            if r == PASSES - 1 and False:
-                load_tokens(HEAD)
+            if r < F_PASSES:
+                load_frames(r)
+            else:
+                load_past(r - F_PASSES)
             load_weight(r)
-        for i in range(HEAD + 0, HEAD + RAW_BUFS):
-            load_tokens(i)
+        for q in range(HEAD // 2, RAW_PAIRS):
+            load_pair(q)
 
-        band_rows = []
-        for name, cols in (("bias", bias_cols), ("gain", gain_cols)):
+        def spread_over_frames(cols, name):
             cols32 = keep.tile([P, PACK], F32, name=name + "_cols32")
             nc.scalar.copy(out=cols32[:], in_=cols[:])
-            bank = turn.tile([P, PACK, P], F32, name="bank")
+            bank = turns.tile([P, PACK, P], F32, name="bank")
             for c in range(PACK):
                 nc.tensor.transpose(bank[:, c, :], cols32[:, c : c + 1].to_broadcast([P, P]), ident[:])
             rows = keep.tile([P, N], F32, name=name + "_rows")
-            nc.vector.tensor_copy(out=rows[:].rearrange("r (p c) -> r p c", c=PACK), in_=bank[:].rearrange("r c p -> r p c"))
-            band_rows.append(rows)
-        bias_rows, gain_rows = band_rows
+            nc.vector.tensor_copy(
+                out=rows[:].rearrange("r (p c) -> r p c", c=PACK), in_=bank[:].rearrange("r c p -> r p c")
+            )
+            return rows
 
-        def head_multiply(r):
-            for i0, g in ((2, r - 1), (0, r)):
-                if 0 <= g < PASSES:
-                    multiply(i0, g)
-                    multiply(i0 + 1, g)
+        bias_rows = spread_over_frames(bias_cols, "bias")
+        gain_rows = spread_over_frames(gain_cols, "gain")
 
-        def sorts(i):
-            if SORT_FROM <= i < TILES:
-                sort_past(i)
-        def ssorts(i):
-            if S_SORT_FROM <= i < TILES:
-                sort_frames(i)
+        def head_round(i, g):
+            if g < F_PASSES:
+                return g + i // 2
+            return max(g, F_PASSES + i) if i < HEAD - 1 else PASSES
+
+        def multiply_head_round(r):
+            due = [(i, g) for i in range(HEAD) for g in range(PASSES) if head_round(i, g) == r]
+            for i, g in [ig for ig in due if ig[1] != r] + [ig for ig in due if ig[1] == r]:
+                multiply(i, g)
 
         for r in range(PASSES):
-            i0, j = 2 * (r % 2), r // 2
-            turn_chunk(i0, j)
-            turn_chunk(i0 + 1, j)
+            if r < F_PASSES:
+                turn_frames(2 * r)
+                turn_frames(2 * r + 1)
+            else:
+                turn_past(r - F_PASSES)
             if r > 0:
-                head_multiply(r - 1)
-            if r == PASSES - 1:
-                quantize_chunk(i0, j)
-                sorts(HEAD)
-                ssorts(HEAD)
-                quantize_chunk(i0 + 1, j)
-            group_weight(r, nc.vector.tensor_copy, slice(0, V_COLS))
-            group_weight(r, nc.scalar.copy, slice(V_COLS, N))
-            if r < PASSES - 1:
-                quantize_chunk(i0, j)
-                quantize_chunk(i0 + 1, j)
+                multiply_head_round(r - 1)
+            group_weight(r)
+            if r < F_PASSES:
+                quantize_frames(2 * r)
+                quantize_frames(2 * r + 1)
+            else:
+                quantize_past(r - F_PASSES)
             quantize_weight(r)
+        for q in range(HEAD // 2):
+            load_pair(RAW_PAIRS + q)
 
-        whole = slice(0, N)
-        finish_at = lambda i: max(i + 3, 5 + i // 2)
+        def epilogue_step(i):
+            return i + 3 + max(0, 2 - i // CATCH_UP)
+
+        last = TILES - 1
+        all_bands = slice(0, N)
         for s in range(HEAD, TILES + 3):
-            done = [i for i in range(TILES - 1) if finish_at(i) == s]
-            late_done = [i for i in range(TILES - 1) if finish_at(i) == s - 1]
-            if True:
-                for i in late_done:
-                    compress_and_store(i, whole)
-            sorts(s + 1)
+            for i in range(last):
+                if epilogue_step(i) == s - 1:
+                    compress_and_store(i, all_bands)
+            if SORT_PAST_FROM <= s + 1 < TILES:
+                sort_past(s + 1)
             if s < TILES:
-                for j in (1, 2, 0):
-                    turn_chunk(s, j)
-            if not True:
-                for i in late_done:
-                    compress_and_store(i, whole)
-            ssorts(s + 1)
-            if s + RAW_BUFS < TILES:
-                load_tokens(s + RAW_BUFS)
-            for i in done:
-                add_bias(i, whole)
+                turn_past(s)
+                turn_frames(s)
+            if SORT_FRAMES_FROM <= s + 1 < TILES:
+                sort_frames(s + 1)
+            if s % 2 == 1 and s // 2 + RAW_PAIRS < PAIRS:
+                load_pair(s // 2 + RAW_PAIRS)
+            due = [i for i in range(last) if epilogue_step(i) == s]
+            for i in due:
+                add_bias(i, all_bands)
             if HEAD <= s - 1 < TILES:
-                quantize_chunk(s - 1, 0)
-            for i in done:
-                floor_and_gain(i, whole)
+                quantize_frames(s - 1)
+            for i in due:
+                floor_and_gain(i, all_bands)
             if HEAD <= s - 1 < TILES:
                 quantize_past(s - 1)
             if s - 2 < HEAD:
-                head_multiply(s + 1)
+                multiply_head_round(s + 1)
             elif s - 2 < TILES:
                 for g in range(PASSES):
                     multiply(s - 2, g)
-        last = TILES - 1
+
         parts = [slice(a * N // TAIL_PARTS, (a + 1) * N // TAIL_PARTS) for a in range(TAIL_PARTS)]
         for a in range(TAIL_PARTS + 1):
             if a < TAIL_PARTS:

@@ -23,38 +23,48 @@ PAIRS = TILES // 2
 F_PASSES = C // K_PASS
 P_PASSES = L // K_PASS
 PASSES = F_PASSES + P_PASSES
+BANKS = 8
 HEAD = 4
+FIRST_PAIR = HEAD // 2
 V_BANDS = 384
-RAW_PAIRS = 4
-RESULT_BUFS = 8
-SORT_PAST_FROM = 5
-SORT_FRAMES_FROM = 8
-CATCH_UP = 6
+RAW_PAIRS = 3
+RESULT_BUFS = 3
 TAIL_PARTS = 4
+ALL_BANDS = slice(0, N)
+BOTH_TILES = slice(0, 2)
+PAST_FIRST = list(range(F_PASSES, PASSES)) + list(range(F_PASSES))
 
 
 def tile_mel_dereverberation_s2_kernel(tc, frames, mel, past, late, bias, gain, out):
     nc = tc.nc
-    frames_by_pair = frames.rearrange("(q r s) k -> q r s k", r=P, s=2)
-    past_by_pair = past.rearrange("(q r s) k -> q r s k", r=P, s=2)
+    frames_by_pair = frames.rearrange("(q r s) k -> q r (s k)", r=P, s=2)
+    past_by_pair = past.rearrange("(q r s) k -> q r (s k)", r=P, s=2)
     out_by_pair = out.rearrange("(q r s) n -> q r s n", r=P, s=2)
 
     with ExitStack() as ctx:
         keep = ctx.enter_context(tc.tile_pool(name="keep", bufs=1))
         raw = ctx.enter_context(tc.tile_pool(name="raw", bufs=RAW_PAIRS))
-        work = ctx.enter_context(tc.tile_pool(name="work", bufs=4))
+        work = ctx.enter_context(tc.tile_pool(name="work", bufs=2))
+        quant = ctx.enter_context(tc.tile_pool(name="quant", bufs=HEAD))
         outs = ctx.enter_context(tc.tile_pool(name="outs", bufs=RESULT_BUFS))
-        turns = ctx.enter_context(tc.psum_pool(name="turns", bufs=4))
-        sums = ctx.enter_context(tc.psum_pool(name="sums", bufs=HEAD))
+        psum = ctx.enter_context(tc.psum_pool(name="psum", bufs=1))
         ctx.enter_context(tc.manual_schedule())
 
         ident = keep.tile([P, P], F32)
         make_identity(nc, ident[:])
 
         w_raw, w_grouped, w_codes, w_scales = {}, {}, {}, {}
-        f_words, p_words, f_grouped, p_grouped = {}, {}, {}, {}
+        f_words, p_words, acc = {}, {}, {}
+        p_raw, f_grouped, p_grouped, biased, gained = {}, {}, {}, {}, {}
         x_codes, x_scales = {}, {}
-        acc, biased, gained = {}, {}, {}
+
+        turn_banks = list(range(HEAD, BANKS))
+
+        def next_turn_bank(shape):
+            b = turn_banks[0]
+            turn_banks.remove(b)
+            turn_banks.append(b)
+            return psum.tile(shape, F32, name="bank%d" % b)
 
         def token_format(g):
             return E4M3 if g < F_PASSES else E5M2
@@ -66,7 +76,7 @@ def tile_mel_dereverberation_s2_kernel(tc, frames, mel, past, late, bias, gain, 
             nc.sync.dma_start(out=w_raw[g][:], in_=rows.rearrange("(p t) n -> p t n", t=PACK))
 
         def group_weight(g):
-            w_grouped[g] = work.tile([P, N, PACK], BF16, name="w_grouped", align_bytes=64, bufs=2)
+            w_grouped[g] = work.tile([P, N, PACK], BF16, name="w_grouped", align_bytes=64)
             for copy, bands in ((nc.vector.tensor_copy, slice(0, V_BANDS)), (nc.scalar.copy, slice(V_BANDS, N))):
                 copy(
                     out=w_grouped[g][:, bands, :].rearrange("p (c i) t -> p c t i", i=4),
@@ -86,33 +96,38 @@ def tile_mel_dereverberation_s2_kernel(tc, frames, mel, past, late, bias, gain, 
             return rows.bitcast(F32).rearrange("r (g m u) -> r g u m", m=P, u=2)
 
         def load_frames(q):
-            f_raw = raw.tile([P, 2, C], BF16, name="f_raw")
+            f_raw = raw.tile([P, 2 * C], BF16, name="f_raw", bufs=RAW_PAIRS + 1)
             nc.sync.dma_start(out=f_raw[:], in_=frames_by_pair[q])
             for s in range(2):
-                f_words[2 * q + s] = words_by_parity(f_raw[:, s, :])
+                f_words[2 * q + s] = words_by_parity(f_raw[:, s * C : (s + 1) * C])
 
-        def load_past(i):
-            p_raw = raw.tile([P, L], BF16, name="p_raw", bufs=2 * RAW_PAIRS)
-            nc.sync.dma_start(out=p_raw[:], in_=past_by_pair[i // 2, :, i % 2, :])
-            p_words[i] = words_by_parity(p_raw[:])
+        def load_past_tile(i):
+            p_tile = raw.tile([P, L], BF16, name="p_tile", bufs=HEAD)
+            nc.sync.dma_start(out=p_tile[:], in_=past_by_pair[i // 2, :, i % 2 * L : (i % 2 + 1) * L])
+            p_words[i] = words_by_parity(p_tile[:])
 
         def load_pair(q):
-            load_past(2 * q)
+            p_raw[q] = raw.tile([P, 2 * L], BF16, name="p_raw")
+            nc.sync.dma_start(out=p_raw[q][:], in_=past_by_pair[q])
             load_frames(q)
-            load_past(2 * q + 1)
 
-        def sort_past(i):
-            p_sorted = work.tile([P, P_PASSES, 2, P], F32, name="p_sorted")
-            nc.vector.tensor_copy(out=p_sorted[:], in_=p_words[i])
-            p_words[i] = p_sorted[:]
+        def sort_words(copy, ordered, by_parity):
+            walk = "r g u (b i) -> r g b u i"
+            copy(out=ordered.rearrange(walk, i=4), in_=by_parity.rearrange(walk, i=4))
+
+        def sort_past(q):
+            p_sorted = work.tile([P, 2 * P_PASSES, 2, P], F32, name="p_sorted")
+            sort_words(nc.vector.tensor_copy, p_sorted[:], words_by_parity(p_raw[q][:]))
+            for s in range(2):
+                p_words[2 * q + s] = p_sorted[:, s * P_PASSES : (s + 1) * P_PASSES, :, :]
 
         def sort_frames(i):
             f_sorted = work.tile([P, F_PASSES, 2, P], F32, name="f_sorted")
-            nc.scalar.copy(out=f_sorted[:], in_=f_words[i])
+            sort_words(nc.scalar.copy, f_sorted[:], f_words[i])
             f_words[i] = f_sorted[:]
 
         def turn_two_passes(words, grouped):
-            bank = turns.tile([P, 2, 2, P], F32, name="bank")
+            bank = next_turn_bank([P, 2, 2, P])
             for g in range(2):
                 for u in range(2):
                     nc.tensor.transpose(bank[:, g, u, :], words[:, g, u, :], ident[:])
@@ -122,62 +137,90 @@ def tile_mel_dereverberation_s2_kernel(tc, frames, mel, past, late, bias, gain, 
             )
 
         def turn_frames(i):
-            f_grouped[i] = work.tile([P, C], BF16, name="f_grouped", align_bytes=64, bufs=3)
-            turn_two_passes(f_words[i], f_grouped[i][:])
+            q, s = divmod(i, 2)
+            if s == 0:
+                f_grouped[q] = work.tile([P, 2 * C], BF16, name="f_grouped", align_bytes=64)
+            turn_two_passes(f_words[i], f_grouped[q][:, s * C : (s + 1) * C])
 
         def turn_past(i):
-            p_grouped[i] = work.tile([P, L], BF16, name="p_grouped", align_bytes=64, bufs=3)
+            q, s = divmod(i, 2)
+            if s == 0:
+                p_grouped[q] = work.tile([P, 2 * L], BF16, name="p_grouped", align_bytes=64)
             for g in range(0, P_PASSES, 2):
-                turn_two_passes(p_words[i][:, g : g + 2, :, :], p_grouped[i][:, g * K_PASS : (g + 2) * K_PASS])
+                k0 = s * L + g * K_PASS
+                turn_two_passes(p_words[i][:, g : g + 2, :, :], p_grouped[q][:, k0 : k0 + 2 * K_PASS])
 
-        def quantize_tokens(i, grouped, first_pass, passes, name):
-            codes = work.tile([P, passes * P], U32, name=name + "_codes", align_bytes=64)
-            scales = work.tile([P, passes * P], U8, name=name + "_scales", align_bytes=64)
-            nc.vector.quantize_mx(out=codes[:].bitcast(token_format(first_pass)), scales=scales[:], in_=grouped[:])
-            for g in range(passes):
-                x_codes[i, first_pass + g] = codes[:, g * P : (g + 1) * P]
-                x_scales[i, first_pass + g] = scales[:, g * P : (g + 1) * P]
+        def turn_tile(i):
+            turn_past(i)
+            turn_frames(i)
 
-        def quantize_frames(i):
-            quantize_tokens(i, f_grouped[i], 0, F_PASSES, "f")
+        def quantize_tokens(tiles, grouped, first_pass, passes, name):
+            q, s = divmod(tiles[0], 2)
+            width = len(tiles) * passes * P
+            codes = quant.tile([P, width], U32, name=name + "_codes", align_bytes=64)
+            scales = quant.tile([P, width], U8, name=name + "_scales", align_bytes=64)
+            k0 = s * passes * K_PASS
+            nc.vector.quantize_mx(
+                out=codes[:].bitcast(token_format(first_pass)),
+                scales=scales[:],
+                in_=grouped[q][:, k0 : k0 + width * PACK],
+            )
+            for n, i in enumerate(tiles):
+                for g in range(passes):
+                    cols = slice((n * passes + g) * P, (n * passes + g + 1) * P)
+                    x_codes[i, first_pass + g] = codes[:, cols]
+                    x_scales[i, first_pass + g] = scales[:, cols]
 
-        def quantize_past(i):
-            quantize_tokens(i, p_grouped[i], F_PASSES, P_PASSES, "p")
+        def quantize_frames(*tiles):
+            quantize_tokens(tiles, f_grouped, 0, F_PASSES, "f")
 
-        def multiply(i, g):
-            if g == 0:
-                acc[i] = sums.tile([P, N], F32, name="acc")
+        def quantize_past(*tiles):
+            quantize_tokens(tiles, p_grouped, F_PASSES, P_PASSES, "p")
+
+        def multiply(i, g, first, last):
+            if g == first:
+                acc[i] = psum.tile([P, N], F32, name="bank%d" % (i if i < HEAD else i % 2))
             nc.tensor.matmul_mx(
                 out=acc[i][:],
                 lhsT=x_codes[i, g].bitcast(token_format(g)),
                 lhsT_scale=x_scales[i, g],
                 rhs=w_codes[g][:].bitcast(E4M3),
                 rhs_scale=w_scales[g][:],
-                start=(g == 0),
-                stop=(g == PASSES - 1),
+                start=(g == first),
+                stop=(g == last),
             )
 
-        def add_bias(i, bands):
-            if bands.start == 0:
-                biased[i] = work.tile([P, N], F32, name="biased")
-            nc.vector.tensor_tensor(out=biased[i][:, bands], in0=acc[i][:, bands], in1=bias_rows[:, bands], op=ALU.add)
+        def multiply_pair(q):
+            for i in (2 * q, 2 * q + 1):
+                for g in PAST_FIRST:
+                    multiply(i, g, PAST_FIRST[0], PAST_FIRST[-1])
 
-        def floor_and_gain(i, bands):
-            if bands.start == 0:
-                gained[i] = work.tile([P, N], F32, name="gained")
+        def add_bias(i, bands=ALL_BANDS):
+            q, s = divmod(i, 2)
+            if s == 0:
+                biased[q] = work.tile([P, 2, N], F32, name="biased", bufs=3)
+            nc.vector.tensor_tensor(out=biased[q][:, s, bands], in0=acc[i][:, bands], in1=bias_rows[:, bands], op=ALU.add)
+
+        def floor_and_gain(q, tiles=BOTH_TILES, bands=ALL_BANDS):
+            if tiles.start == 0:
+                gained[q] = work.tile([P, 2, N], F32, name="gained")
+            shape = [P, tiles.stop - tiles.start, bands.stop - bands.start]
             nc.vector.scalar_tensor_tensor(
-                out=gained[i][:, bands],
-                in0=biased[i][:, bands],
+                out=gained[q][:, tiles, bands],
+                in0=biased[q][:, tiles, bands],
                 scalar=0.0,
-                in1=gain_rows[:, bands],
+                in1=gain_rows[:, bands].unsqueeze(1).to_broadcast(shape),
                 op0=ALU.max,
                 op1=ALU.mult,
             )
 
-        def compress_and_store(i, bands):
-            result = outs.tile([P, bands.stop - bands.start], F32, name="result")
-            nc.scalar.activation(out=result[:], in_=gained[i][:, bands], func=ACT.Ln, bias=1.0)
-            nc.sync.dma_start(out=out_by_pair[i // 2, :, i % 2, bands], in_=result[:])
+        def compress_and_store(q, result, tiles=BOTH_TILES, bands=ALL_BANDS):
+            nc.scalar.activation(out=result, in_=gained[q][:, tiles, bands], func=ACT.Ln, bias=1.0)
+            nc.sync.dma_start(out=out_by_pair[q, :, tiles, bands], in_=result)
+
+        def compress_and_store_pair(q):
+            result = outs.tile([P, 2, N], F32, name="result")
+            compress_and_store(q, result[:])
 
         bias_cols = keep.tile([P, PACK], BF16)
         nc.scalar.dma_start(out=bias_cols[:], in_=bias.rearrange("(p c) -> p c", c=PACK))
@@ -188,19 +231,19 @@ def tile_mel_dereverberation_s2_kernel(tc, frames, mel, past, late, bias, gain, 
         nc.vector.memset(warm[:], 0.0)
         nc.scalar.activation(out=warm[:], in_=warm[:], func=ACT.Ln, bias=1.0)
 
+        load_weight(0)
         for r in range(PASSES):
             if r < F_PASSES:
                 load_frames(r)
             else:
-                load_past(r - F_PASSES)
-            load_weight(r)
-        for q in range(HEAD // 2, RAW_PAIRS):
-            load_pair(q)
+                load_past_tile(r - F_PASSES)
+            if r > 0:
+                load_weight(r)
 
         def spread_over_frames(cols, name):
             cols32 = keep.tile([P, PACK], F32, name=name + "_cols32")
             nc.scalar.copy(out=cols32[:], in_=cols[:])
-            bank = turns.tile([P, PACK, P], F32, name="bank")
+            bank = next_turn_bank([P, PACK, P])
             for c in range(PACK):
                 nc.tensor.transpose(bank[:, c, :], cols32[:, c : c + 1].to_broadcast([P, P]), ident[:])
             rows = keep.tile([P, N], F32, name=name + "_rows")
@@ -220,63 +263,87 @@ def tile_mel_dereverberation_s2_kernel(tc, frames, mel, past, late, bias, gain, 
         def multiply_head_round(r):
             due = [(i, g) for i in range(HEAD) for g in range(PASSES) if head_round(i, g) == r]
             for i, g in [ig for ig in due if ig[1] != r] + [ig for ig in due if ig[1] == r]:
-                multiply(i, g)
+                multiply(i, g, 0, PASSES - 1)
 
+        group_weight(0)
+        quantize_weight(0)
         for r in range(PASSES):
             if r < F_PASSES:
                 turn_frames(2 * r)
                 turn_frames(2 * r + 1)
             else:
                 turn_past(r - F_PASSES)
+            if r == F_PASSES + 1:
+                load_past_tile(HEAD)
+                load_frames(FIRST_PAIR)
+                load_past_tile(HEAD + 1)
+                for q in range(FIRST_PAIR + 1, FIRST_PAIR + 1 + RAW_PAIRS):
+                    load_pair(q)
             if r > 0:
                 multiply_head_round(r - 1)
-            group_weight(r)
+                group_weight(r)
             if r < F_PASSES:
                 quantize_frames(2 * r)
                 quantize_frames(2 * r + 1)
             else:
                 quantize_past(r - F_PASSES)
-            quantize_weight(r)
-        for q in range(HEAD // 2):
-            load_pair(RAW_PAIRS + q)
+            if r > 0:
+                quantize_weight(r)
 
-        def epilogue_step(i):
-            return i + 3 + max(0, 2 - i // CATCH_UP)
+        turn_tile(HEAD)
+        multiply_head_round(PASSES - 1)
+        quantize_past(HEAD)
+        add_bias(0)
+        add_bias(1)
+        turn_tile(HEAD + 1)
+        multiply_head_round(PASSES)
+        sort_past(FIRST_PAIR + 1)
+        add_bias(2)
+        add_bias(3)
+        turn_banks.extend(range(2, HEAD))
+        quantize_past(HEAD + 1)
+        quantize_frames(HEAD, HEAD + 1)
+        floor_and_gain(0)
 
-        last = TILES - 1
-        all_bands = slice(0, N)
-        for s in range(HEAD, TILES + 3):
-            for i in range(last):
-                if epilogue_step(i) == s - 1:
-                    compress_and_store(i, all_bands)
-            if SORT_PAST_FROM <= s + 1 < TILES:
-                sort_past(s + 1)
-            if s < TILES:
-                turn_past(s)
-                turn_frames(s)
-            if SORT_FRAMES_FROM <= s + 1 < TILES:
-                sort_frames(s + 1)
-            if s % 2 == 1 and s // 2 + RAW_PAIRS < PAIRS:
-                load_pair(s // 2 + RAW_PAIRS)
-            due = [i for i in range(last) if epilogue_step(i) == s]
-            for i in due:
-                add_bias(i, all_bands)
-            if HEAD <= s - 1 < TILES:
-                quantize_frames(s - 1)
-            for i in due:
-                floor_and_gain(i, all_bands)
-            if HEAD <= s - 1 < TILES:
-                quantize_past(s - 1)
-            if s - 2 < HEAD:
-                multiply_head_round(s + 1)
-            elif s - 2 < TILES:
-                for g in range(PASSES):
-                    multiply(s - 2, g)
+        last = PAIRS - 1
+        for q in range(FIRST_PAIR + 1, PAIRS):
+            turn_tile(2 * q)
+            turn_tile(2 * q + 1)
+            if q + RAW_PAIRS < PAIRS:
+                load_pair(q + RAW_PAIRS)
+            if q == FIRST_PAIR + 1:
+                compress_and_store_pair(0)
+            else:
+                add_bias(2 * (q - 2) + 1)
+            if q < last:
+                sort_past(q + 1)
+            else:
+                quantize_past(2 * q)
+            floor_and_gain(q - 2)
+            compress_and_store_pair(q - 2)
+            if q < last:
+                sort_frames(2 * (q + 1) + 1)
+            multiply_pair(q - 1)
+            if q < last:
+                quantize_past(2 * q, 2 * q + 1)
+            else:
+                quantize_past(2 * q + 1)
+            add_bias(2 * (q - 1))
+            quantize_frames(2 * q, 2 * q + 1)
 
+        add_bias(2 * (last - 1) + 1)
+        multiply_pair(last)
+        floor_and_gain(last - 1)
+        compress_and_store_pair(last - 1)
+        last_result = keep.tile([P, 2, N], F32)
+        first_tile, second_tile = slice(0, 1), slice(1, 2)
+        add_bias(2 * last)
+        floor_and_gain(last, first_tile)
+        compress_and_store(last, last_result[:, first_tile, :], first_tile)
         parts = [slice(a * N // TAIL_PARTS, (a + 1) * N // TAIL_PARTS) for a in range(TAIL_PARTS)]
         for a in range(TAIL_PARTS + 1):
             if a < TAIL_PARTS:
-                add_bias(last, parts[a])
+                add_bias(2 * last + 1, parts[a])
             if a > 0:
-                floor_and_gain(last, parts[a - 1])
-                compress_and_store(last, parts[a - 1])
+                floor_and_gain(last, second_tile, parts[a - 1])
+                compress_and_store(last, last_result[:, second_tile, parts[a - 1]], second_tile, parts[a - 1])

from contextlib import ExitStack

import concourse.mybir as mybir
from concourse.masks import make_identity

T, C, L, N = 2048, 1024, 2048, 512
FLOPS = 2 * T * (C + L) * N

F32 = mybir.dt.float32
BF16 = mybir.dt.bfloat16
U32 = mybir.dt.uint32
U8 = mybir.dt.uint8
E4M3 = mybir.dt.float8_e4m3fn_x4
E5M2 = mybir.dt.float8_e5m2_x4
ALU = mybir.AluOpType
ACT = mybir.ActivationFunctionType

P = 128
PACK = 4
K_PASS = P * PACK
TILES = T // P
PAIRS = TILES // 2
F_PASSES = C // K_PASS
P_PASSES = L // K_PASS
PASSES = F_PASSES + P_PASSES
BANKS = 8
HEAD = 4
FIRST_PAIR = HEAD // 2
V_BANDS = 384
RAW_PAIRS = 3
RESULT_BUFS = 3
TAIL_PARTS = 4
ALL_BANDS = slice(0, N)
BOTH_TILES = slice(0, 2)
PAST_FIRST = list(range(F_PASSES, PASSES)) + list(range(F_PASSES))


def tile_mel_dereverberation_s2_kernel(tc, frames, mel, past, late, bias, gain, out):
    nc = tc.nc
    frames_by_pair = frames.rearrange("(q r s) k -> q r (s k)", r=P, s=2)
    past_by_pair = past.rearrange("(q r s) k -> q r (s k)", r=P, s=2)
    out_by_pair = out.rearrange("(q r s) n -> q r s n", r=P, s=2)

    with ExitStack() as ctx:
        keep = ctx.enter_context(tc.tile_pool(name="keep", bufs=1))
        raw = ctx.enter_context(tc.tile_pool(name="raw", bufs=RAW_PAIRS))
        work = ctx.enter_context(tc.tile_pool(name="work", bufs=2))
        quant = ctx.enter_context(tc.tile_pool(name="quant", bufs=HEAD))
        outs = ctx.enter_context(tc.tile_pool(name="outs", bufs=RESULT_BUFS))
        psum = ctx.enter_context(tc.psum_pool(name="psum", bufs=1))
        ctx.enter_context(tc.manual_schedule())

        ident = keep.tile([P, P], F32)
        make_identity(nc, ident[:])

        w_raw, w_grouped, w_codes, w_scales = {}, {}, {}, {}
        f_words, p_words, acc = {}, {}, {}
        p_raw, f_grouped, p_grouped, biased, gained = {}, {}, {}, {}, {}
        x_codes, x_scales = {}, {}

        turn_banks = list(range(HEAD, BANKS))

        def next_turn_bank(shape):
            b = turn_banks[0]
            turn_banks.remove(b)
            turn_banks.append(b)
            return psum.tile(shape, F32, name="bank%d" % b)

        def token_format(g):
            return E4M3 if g < F_PASSES else E5M2

        def load_weight(g):
            src, g_src = (mel, g) if g < F_PASSES else (late, g - F_PASSES)
            rows = src[g_src * K_PASS : (g_src + 1) * K_PASS, :]
            w_raw[g] = keep.tile([P, PACK, N], BF16, name="w_raw%d" % g)
            nc.sync.dma_start(out=w_raw[g][:], in_=rows.rearrange("(p t) n -> p t n", t=PACK))

        def group_weight(g):
            w_grouped[g] = work.tile([P, N, PACK], BF16, name="w_grouped", align_bytes=64)
            for copy, bands in ((nc.vector.tensor_copy, slice(0, V_BANDS)), (nc.scalar.copy, slice(V_BANDS, N))):
                copy(
                    out=w_grouped[g][:, bands, :].rearrange("p (c i) t -> p c t i", i=4),
                    in_=w_raw[g][:, :, bands].rearrange("p t (c i) -> p c t i", i=4),
                )

        def quantize_weight(g):
            w_codes[g] = keep.tile([P, N], U32, name="w_codes%d" % g, align_bytes=64)
            w_scales[g] = keep.tile([P, N], U8, name="w_scales%d" % g, align_bytes=64)
            nc.vector.quantize_mx(
                out=w_codes[g][:].bitcast(E4M3),
                scales=w_scales[g][:],
                in_=w_grouped[g][:].rearrange("p n t -> p (n t)"),
            )

        def words_by_parity(rows):
            return rows.bitcast(F32).rearrange("r (g m u) -> r g u m", m=P, u=2)

        def load_frames(q):
            f_raw = raw.tile([P, 2 * C], BF16, name="f_raw", bufs=RAW_PAIRS + 1)
            nc.sync.dma_start(out=f_raw[:], in_=frames_by_pair[q])
            for s in range(2):
                f_words[2 * q + s] = words_by_parity(f_raw[:, s * C : (s + 1) * C])

        def load_past_tile(i):
            p_tile = raw.tile([P, L], BF16, name="p_tile", bufs=HEAD)
            nc.sync.dma_start(out=p_tile[:], in_=past_by_pair[i // 2, :, i % 2 * L : (i % 2 + 1) * L])
            p_words[i] = words_by_parity(p_tile[:])

        def load_pair(q):
            p_raw[q] = raw.tile([P, 2 * L], BF16, name="p_raw")
            nc.sync.dma_start(out=p_raw[q][:], in_=past_by_pair[q])
            load_frames(q)

        def sort_words(copy, ordered, by_parity):
            walk = "r g u (b i) -> r g b u i"
            copy(out=ordered.rearrange(walk, i=4), in_=by_parity.rearrange(walk, i=4))

        def sort_past(q):
            p_sorted = work.tile([P, 2 * P_PASSES, 2, P], F32, name="p_sorted")
            sort_words(nc.vector.tensor_copy, p_sorted[:], words_by_parity(p_raw[q][:]))
            for s in range(2):
                p_words[2 * q + s] = p_sorted[:, s * P_PASSES : (s + 1) * P_PASSES, :, :]

        def sort_frames(i):
            f_sorted = work.tile([P, F_PASSES, 2, P], F32, name="f_sorted")
            sort_words(nc.scalar.copy, f_sorted[:], f_words[i])
            f_words[i] = f_sorted[:]

        def turn_two_passes(words, grouped):
            bank = next_turn_bank([P, 2, 2, P])
            for g in range(2):
                for u in range(2):
                    nc.tensor.transpose(bank[:, g, u, :], words[:, g, u, :], ident[:])
            nc.scalar.copy(
                out=grouped.bitcast(F32).rearrange("p (g r u) -> p g r u", g=2, u=2),
                in_=bank[:].rearrange("p g u r -> p g r u"),
            )

        def turn_frames(i):
            q, s = divmod(i, 2)
            if s == 0:
                f_grouped[q] = work.tile([P, 2 * C], BF16, name="f_grouped", align_bytes=64)
            turn_two_passes(f_words[i], f_grouped[q][:, s * C : (s + 1) * C])

        def turn_past(i):
            q, s = divmod(i, 2)
            if s == 0:
                p_grouped[q] = work.tile([P, 2 * L], BF16, name="p_grouped", align_bytes=64)
            for g in range(0, P_PASSES, 2):
                k0 = s * L + g * K_PASS
                turn_two_passes(p_words[i][:, g : g + 2, :, :], p_grouped[q][:, k0 : k0 + 2 * K_PASS])

        def turn_tile(i):
            turn_past(i)
            turn_frames(i)

        def quantize_tokens(tiles, grouped, first_pass, passes, name):
            q, s = divmod(tiles[0], 2)
            width = len(tiles) * passes * P
            codes = quant.tile([P, width], U32, name=name + "_codes", align_bytes=64)
            scales = quant.tile([P, width], U8, name=name + "_scales", align_bytes=64)
            k0 = s * passes * K_PASS
            nc.vector.quantize_mx(
                out=codes[:].bitcast(token_format(first_pass)),
                scales=scales[:],
                in_=grouped[q][:, k0 : k0 + width * PACK],
            )
            for n, i in enumerate(tiles):
                for g in range(passes):
                    cols = slice((n * passes + g) * P, (n * passes + g + 1) * P)
                    x_codes[i, first_pass + g] = codes[:, cols]
                    x_scales[i, first_pass + g] = scales[:, cols]

        def quantize_frames(*tiles):
            quantize_tokens(tiles, f_grouped, 0, F_PASSES, "f")

        def quantize_past(*tiles):
            quantize_tokens(tiles, p_grouped, F_PASSES, P_PASSES, "p")

        def multiply(i, g, first, last):
            if g == first:
                acc[i] = psum.tile([P, N], F32, name="bank%d" % (i if i < HEAD else i % 2))
            nc.tensor.matmul_mx(
                out=acc[i][:],
                lhsT=x_codes[i, g].bitcast(token_format(g)),
                lhsT_scale=x_scales[i, g],
                rhs=w_codes[g][:].bitcast(E4M3),
                rhs_scale=w_scales[g][:],
                start=(g == first),
                stop=(g == last),
            )

        def multiply_pair(q):
            for i in (2 * q, 2 * q + 1):
                for g in PAST_FIRST:
                    multiply(i, g, PAST_FIRST[0], PAST_FIRST[-1])

        def add_bias(i, bands=ALL_BANDS):
            q, s = divmod(i, 2)
            if s == 0:
                biased[q] = work.tile([P, 2, N], F32, name="biased", bufs=3)
            nc.vector.tensor_tensor(out=biased[q][:, s, bands], in0=acc[i][:, bands], in1=bias_rows[:, bands], op=ALU.add)

        def floor_and_gain(q, tiles=BOTH_TILES, bands=ALL_BANDS):
            if tiles.start == 0:
                gained[q] = work.tile([P, 2, N], F32, name="gained")
            shape = [P, tiles.stop - tiles.start, bands.stop - bands.start]
            nc.vector.scalar_tensor_tensor(
                out=gained[q][:, tiles, bands],
                in0=biased[q][:, tiles, bands],
                scalar=0.0,
                in1=gain_rows[:, bands].unsqueeze(1).to_broadcast(shape),
                op0=ALU.max,
                op1=ALU.mult,
            )

        def compress_and_store(q, result, tiles=BOTH_TILES, bands=ALL_BANDS):
            nc.scalar.activation(out=result, in_=gained[q][:, tiles, bands], func=ACT.Ln, bias=1.0)
            nc.sync.dma_start(out=out_by_pair[q, :, tiles, bands], in_=result)

        def compress_and_store_pair(q):
            result = outs.tile([P, 2, N], F32, name="result")
            compress_and_store(q, result[:])

        bias_cols = keep.tile([P, PACK], BF16)
        nc.scalar.dma_start(out=bias_cols[:], in_=bias.rearrange("(p c) -> p c", c=PACK))
        gain_cols = keep.tile([P, PACK], BF16)
        nc.scalar.dma_start(out=gain_cols[:], in_=gain.rearrange("(p c) -> p c", c=PACK))

        warm = keep.tile([P, 1], F32)
        nc.vector.memset(warm[:], 0.0)
        nc.scalar.activation(out=warm[:], in_=warm[:], func=ACT.Ln, bias=1.0)

        load_weight(0)
        for r in range(PASSES):
            if r < F_PASSES:
                load_frames(r)
            else:
                load_past_tile(r - F_PASSES)
            if r > 0:
                load_weight(r)

        def spread_over_frames(cols, name):
            cols32 = keep.tile([P, PACK], F32, name=name + "_cols32")
            nc.scalar.copy(out=cols32[:], in_=cols[:])
            bank = next_turn_bank([P, PACK, P])
            for c in range(PACK):
                nc.tensor.transpose(bank[:, c, :], cols32[:, c : c + 1].to_broadcast([P, P]), ident[:])
            rows = keep.tile([P, N], F32, name=name + "_rows")
            nc.vector.tensor_copy(
                out=rows[:].rearrange("r (p c) -> r p c", c=PACK), in_=bank[:].rearrange("r c p -> r p c")
            )
            return rows

        bias_rows = spread_over_frames(bias_cols, "bias")
        gain_rows = spread_over_frames(gain_cols, "gain")

        def head_round(i, g):
            if g < F_PASSES:
                return g + i // 2
            return max(g, F_PASSES + i) if i < HEAD - 1 else PASSES

        def multiply_head_round(r):
            due = [(i, g) for i in range(HEAD) for g in range(PASSES) if head_round(i, g) == r]
            for i, g in [ig for ig in due if ig[1] != r] + [ig for ig in due if ig[1] == r]:
                multiply(i, g, 0, PASSES - 1)

        group_weight(0)
        quantize_weight(0)
        for r in range(PASSES):
            if r < F_PASSES:
                turn_frames(2 * r)
                turn_frames(2 * r + 1)
            else:
                turn_past(r - F_PASSES)
            if r == F_PASSES + 1:
                load_past_tile(HEAD)
                load_frames(FIRST_PAIR)
                load_past_tile(HEAD + 1)
                for q in range(FIRST_PAIR + 1, FIRST_PAIR + 1 + RAW_PAIRS):
                    load_pair(q)
            if r > 0:
                multiply_head_round(r - 1)
                group_weight(r)
            if r < F_PASSES:
                quantize_frames(2 * r)
                quantize_frames(2 * r + 1)
            else:
                quantize_past(r - F_PASSES)
            if r > 0:
                quantize_weight(r)

        turn_tile(HEAD)
        multiply_head_round(PASSES - 1)
        quantize_past(HEAD)
        add_bias(0)
        add_bias(1)
        turn_tile(HEAD + 1)
        multiply_head_round(PASSES)
        sort_past(FIRST_PAIR + 1)
        add_bias(2)
        add_bias(3)
        turn_banks.extend(range(2, HEAD))
        quantize_past(HEAD + 1)
        quantize_frames(HEAD, HEAD + 1)
        floor_and_gain(0)

        last = PAIRS - 1
        for q in range(FIRST_PAIR + 1, PAIRS):
            turn_tile(2 * q)
            turn_tile(2 * q + 1)
            if q + RAW_PAIRS < PAIRS:
                load_pair(q + RAW_PAIRS)
            if q == FIRST_PAIR + 1:
                compress_and_store_pair(0)
            else:
                add_bias(2 * (q - 2) + 1)
            if q < last:
                sort_past(q + 1)
            else:
                quantize_past(2 * q)
            floor_and_gain(q - 2)
            compress_and_store_pair(q - 2)
            if q < last:
                sort_frames(2 * (q + 1) + 1)
            multiply_pair(q - 1)
            if q < last:
                quantize_past(2 * q, 2 * q + 1)
            else:
                quantize_past(2 * q + 1)
            add_bias(2 * (q - 1))
            quantize_frames(2 * q, 2 * q + 1)

        add_bias(2 * (last - 1) + 1)
        multiply_pair(last)
        floor_and_gain(last - 1)
        compress_and_store_pair(last - 1)
        last_result = keep.tile([P, 2, N], F32)
        first_tile, second_tile = slice(0, 1), slice(1, 2)
        add_bias(2 * last)
        floor_and_gain(last, first_tile)
        compress_and_store(last, last_result[:, first_tile, :], first_tile)
        parts = [slice(a * N // TAIL_PARTS, (a + 1) * N // TAIL_PARTS) for a in range(TAIL_PARTS)]
        for a in range(TAIL_PARTS + 1):
            if a < TAIL_PARTS:
                add_bias(2 * last + 1, parts[a])
            if a > 0:
                floor_and_gain(last, second_tile, parts[a - 1])
                compress_and_store(last, last_result[:, second_tile, parts[a - 1]], second_tile, parts[a - 1])
